import numpy as np
import ml_dtypes


def mxq(x, axis, fmt="e4m3"):
    dtype, down = {"e4m3": (ml_dtypes.float8_e4m3fn, 7), "e5m2": (ml_dtypes.float8_e5m2, 14)}[fmt]
    v = np.moveaxis(np.asarray(x, np.float32).astype(ml_dtypes.bfloat16).astype(np.float64), axis, -1)
    blocks = v.reshape(v.shape[:-1] + (-1, 32))
    amax = np.abs(blocks).max(-1, keepdims=True)
    byte = np.maximum(np.where(amax > 0, np.frexp(amax)[1] - 1 + 127, 0) - down, 1)
    scale = np.exp2(byte - 127.0)
    codes = (blocks / scale).astype(np.float32).astype(dtype).astype(np.float64)
    return np.moveaxis((codes * scale).reshape(v.shape), -1, axis)


WIDE = False


def mx_kscale(k):
    if not WIDE:
        return np.ones(k)
    levels = np.array([30, -30])
    if k % 512:
        return np.exp2(np.random.permutation(np.resize(levels, k // 32))).repeat(32)
    a = np.empty((k // 512, 16))
    for p in range(k // 512):
        a[p, :8] = np.random.permutation(np.resize(levels, 8))
        for g in range(8):
            far = levels[np.abs(levels - a[p, g]) >= 10]
            a[p, g + 8] = far[np.random.randint(len(far))]
    return np.exp2(a.ravel()).repeat(32)


def f64(x):
    return np.asarray(x).astype(np.float64)


def striped(idx):
    return np.tile(idx.reshape(-1, 16).T, (8, 1)).astype(np.uint16)


def unstriped(offs):
    return offs[:16].T.reshape(-1).astype(np.int64)


E2M1 = np.array([0.0, 0.5, 1.0, 1.5, 2.0, 3.0, 4.0, 6.0, -0.0, -0.5, -1.0, -1.5, -2.0, -3.0, -4.0, -6.0])


def pack_weight(w, fmt):
    k, n = w.shape
    w = f64(np.asarray(w, np.float32).astype(ml_dtypes.bfloat16)).reshape(k // 32, 32, n)
    amax = np.abs(w).max(1)
    if fmt == "e4m3":
        byte = np.frexp(amax)[1] - 1 + 127 - 7
    elif fmt == "e5m2":
        byte = np.frexp(amax)[1] - 1 + 127 - 14
    else:
        mant, ex = np.frexp(amax / 6.0)
        byte = np.where(mant > 0.5, ex, ex - 1) + 127
    byte = np.clip(np.where(amax > 0, byte, 1), 1, 254)
    scaled = (w * np.exp2(127.0 - byte)[:, None, :]).reshape(k, n).astype(np.float32)
    by_word = np.ascontiguousarray(scaled.reshape(k // 512, 128, 4, n).transpose(0, 1, 3, 2))
    if fmt == "e4m3":
        words = by_word.astype(ml_dtypes.float8_e4m3fn).view(np.uint8)
    elif fmt == "e5m2":
        words = by_word.astype(ml_dtypes.float8_e5m2).view(np.uint8)
    else:
        c = by_word.astype(ml_dtypes.float4_e2m1fn).view(np.uint8) & 0xF
        words = (c[..., 0::2] | (c[..., 1::2] << 4)).reshape(k // 512, 128, 2 * n)
    return np.ascontiguousarray(words), np.ascontiguousarray(byte.astype(np.uint8).reshape(k // 512, 16, n))


def unpack_weight(words, scales, fmt):
    g, _, n = scales.shape
    words = np.ascontiguousarray(words).reshape(g, 128, n, -1)
    if fmt == "e4m3":
        vals = words.view(ml_dtypes.float8_e4m3fn).astype(np.float64)
    elif fmt == "e5m2":
        vals = words.view(ml_dtypes.float8_e5m2).astype(np.float64)
    else:
        nib = np.empty((g, 128, n, 4), np.uint8)
        nib[..., 0::2] = words & 0xF
        nib[..., 1::2] = words >> 4
        vals = E2M1[nib]
    vals = vals * np.repeat(np.exp2(scales.astype(np.float64) - 127.0), 8, axis=1)[..., None]
    return vals.transpose(0, 1, 3, 2).reshape(g * 512, n)


K, T, E, C, N = 128, 1024, 6, 512, 1536
TOP = 3


def by_expert(wq, xq):
    return np.concatenate([wq[e].T @ xq[:, e * C:(e + 1) * C] for e in range(E)], axis=1)


def setup_inputs():
    n = np.random.standard_normal
    s = mx_kscale(N)[:, None]
    deal = np.repeat(np.arange(E), C).reshape(TOP, T)[:, np.random.permutation(T)]
    deal = np.take_along_axis(deal, np.argsort(np.random.rand(TOP, T), axis=0), axis=0)
    for _ in range(8):
        s_, t_ = np.random.permutation(T).reshape(2, -1); r = np.random.randint(TOP, size=T // 2); x, y = deal[r, s_].copy(), deal[r, t_].copy()
        ok = ~((deal[:, s_] == y).any(0) | (deal[:, t_] == x).any(0)); deal[r[ok], s_[ok]] = y[ok]; deal[r[ok], t_[ok]] = x[ok]
    order = np.lexsort((np.random.rand(TOP * T), deal.reshape(-1)))
    slot_token = order % T; pos = np.empty(TOP * T, np.int64); pos[order] = np.arange(TOP * T); pos = pos.reshape(TOP, T)
    g = np.random.uniform(0.5, 1.5, (TOP, T)); g = g / g.sum(0)
    w_slot = np.empty(E * C)
    for r in range(TOP): w_slot[pos[r]] = g[r]
    dy = pack_weight(n((N, T)) * s, "e5m2")
    return {
        "dy_words": dy[0],
        "dy_scales": dy[1],
        "w": (n((E + 1, N, K)) / np.sqrt(N) / s[None]).astype(np.float32),
        "gate": np.tile(w_slot, (K, 1)).astype(np.float32),
        "offs": striped(slot_token),
        "pos1": striped(pos[0]),
        "pos2": striped(pos[1]),
        "pos3": striped(pos[2]),
    }


def reference(dy_words, dy_scales, w, gate, offs, pos1, pos2, pos3):
    idx = unstriped(offs)
    gq = unpack_weight(dy_words, dy_scales, "e5m2")[:, idx]
    wq = mxq(f64(w), 1, "e4m3")
    ds = wq[E].T @ unpack_weight(dy_words, dy_scales, "e5m2")
    dx = f64(gate) * by_expert(wq, gq)
    return ds + dx[:, unstriped(pos1)] + dx[:, unstriped(pos2)] + dx[:, unstriped(pos3)]

@@ -1,0 +1,171 @@
+from contextlib import ExitStack
+
+import concourse.mybir as mybir
+
+K, T, E, C, N = 128, 1024, 6, 512, 1536
+P = 128
+PACK = 4
+PASSES = 3
+SLOTS = E * C
+FLOPS = 2 * K * N * (SLOTS + T)
+
+F32 = mybir.dt.float32
+BF16 = mybir.dt.bfloat16
+I32 = mybir.dt.int32
+U32 = mybir.dt.uint32
+U16 = mybir.dt.uint16
+U8 = mybir.dt.uint8
+E4M3 = mybir.dt.float8_e4m3fn_x4
+E5M2 = mybir.dt.float8_e5m2_x4
+MULT = mybir.AluOpType.mult
+ADD = mybir.AluOpType.add
+
+USE_POOL = True
+SHIFT_ROWS = 112
+SCALE_PIECE = 768
+PIECES = [(0, 512), (512, 1024)]
+
+
+def tile_moe_bds_lin_none_kernel(tc, dy_words, dy_scales, w, gate, offs, pos1, pos2, pos3, out):
+    nc = tc.nc
+    with ExitStack() as ctx:
+        lists = ctx.enter_context(tc.tile_pool(name="lists", bufs=1))
+        keep = ctx.enter_context(tc.tile_pool(name="keep", bufs=1))
+        reuse = ctx.enter_context(tc.tile_pool(name="reuse", bufs=1))
+        psum = ctx.enter_context(tc.psum_pool(name="psum", bufs=1))
+
+        offs_sb = lists.tile([P, SLOTS // 16], U16, name="offs_sb")
+        pos_sb = [lists.tile([P, T // 16], U16, name="pos%d_sb" % r) for r in range(3)]
+        words = [keep.tile([P, T], I32, name="words%d" % a, align_bytes=64) for a in range(PASSES)]
+        packed = keep.tile([P, T], U8, name="packed", align_bytes=64)
+        tok_plane = [packed] + [keep.tile([P, T], U8, name="tok_plane%d" % a, align_bytes=64) for a in (1, 2)]
+        gathered_scales = keep.tile([P, SLOTS], U8, name="gathered_scales", align_bytes=64)
+        slot_plane = [gathered_scales] + [keep.tile([P, SLOTS], U8, name="slot_plane%d" % a, align_bytes=64) for a in (1, 2)]
+        raw_bytes = PASSES * PACK * K * 4
+        w_raw = [reuse.tile([P, PASSES, PACK, K], F32, name="w_raw%d" % e, align_bytes=64, offset=e * raw_bytes) for e in range(E + 1)]
+        first = [keep.tile([P, C], U32, name="slot_first%d" % e, align_bytes=64) for e in range(E)]
+        rest = [reuse.tile([P, 2, C], U32, name="slot_rest%d" % e, align_bytes=64, offset=e * raw_bytes) for e in range(E)]
+        slot_words = [[first[e][:], rest[e][:, 0, :], rest[e][:, 1, :]] for e in range(E)]
+        w_bf = [keep.tile([P, PASSES * K * PACK], BF16, name="w_bf%d" % e, align_bytes=64) for e in range(E + 1)]
+        w_codes = [keep.tile([P, PASSES * K], U32, name="w_codes%d" % e, align_bytes=64) for e in range(E)]
+        w_codes.append(reuse.tile([P, PASSES * K], U32, name="w_codes_shared", align_bytes=64, offset=(E - 1) * raw_bytes + 2 * C * 4))
+        w_scales = [keep.tile([P, PASSES * K], U8, name="w_scales%d" % e, align_bytes=64) for e in range(E + 1)]
+        gate_sb = [keep.tile([P, SLOTS // 2], F32, name="gate%d" % h) for h in range(2)]
+        sums_all = reuse.tile([P, E - 1, C], F32, name="sums_all", align_bytes=64, offset=E * raw_bytes)
+        sums = [sums_all[:, e, :] for e in range(E - 1)]
+        dx = keep.tile([P, SLOTS], F32, name="dx")
+        ds = keep.tile([P, T], F32, name="ds")
+        acc = [psum.tile([P, C], F32, name="acc%d" % e) for e in range(E)]
+        acc_s = [psum.tile([P, C], F32, name="acc_s%d" % h) for h in range(2)]
+
+        nc.gpsimd.memset(packed[:].bitcast(I32), 0)
+        nc.sync.dma_start(offs_sb[:], offs)
+        for a in range(PASSES):
+            nc.sync.dma_start(words[a][:], dy_words[a].rearrange("p t d -> p (t d)").bitcast(I32))
+        for q in range(4):
+            nc.scalar.dma_start(packed[32 * q : 32 * q + 12, :].bitcast(I32), dy_scales[:, 4 * q : 4 * q + 4, :].bitcast(I32))
+        for a in (1, 2):
+            nc.gpsimd.memset(slot_plane[a][:].bitcast(I32), 0)
+            nc.gpsimd.memset(tok_plane[a][:].bitcast(I32), 0)
+
+        def load_w(e):
+            nc.sync.dma_start(w_raw[e][:], w[e].rearrange("(a p j) k -> p a j k", a=PASSES, j=PACK))
+
+        def load_gate(h):
+            nc.sync.dma_start(gate_sb[h][:], gate[:, h * (SLOTS // 2) : (h + 1) * (SLOTS // 2)])
+
+        for e in range(E + 1):
+            load_w(e)
+        load_gate(0)
+        load_gate(1)
+        for r, pos in enumerate((pos1, pos2, pos3)):
+            nc.sync.dma_start(pos_sb[r][:], pos)
+
+        def shift(queue, dst, src, a):
+            queue.dma_start(dst[0:SHIFT_ROWS, :].bitcast(I32), src[4 * a : 4 * a + SHIFT_ROWS, :].bitcast(I32))
+
+        for a in (1, 2):
+            shift(nc.gpsimd, tok_plane[a], packed, a)
+
+        def cast(e):
+            nc.scalar.copy(w_bf[e][:].rearrange("p (a k j) -> p a k j", a=PASSES, j=PACK), w_raw[e][:].rearrange("p a j k -> p a k j"))
+
+        def quantise(e):
+            for lo, hi in ((0, 2 * K), (2 * K, 3 * K)):
+                nc.vector.quantize_mx(out=w_codes[e][:, lo:hi].bitcast(E4M3), scales=w_scales[e][:, lo:hi], in_=w_bf[e][:, PACK * lo : PACK * hi])
+
+        def gather_words(e, a):
+            nc.vector.tensor_copy(slot_words[e][a], words[a][:].bitcast(U32).indirect(offs_sb[:, e * C // 16 : (e + 1) * C // 16]))
+
+        def multiply(e):
+            for a in range(PASSES):
+                nc.tensor.matmul_mx(
+                    out=acc[e][:],
+                    lhsT=w_codes[e][:, a * K : (a + 1) * K].bitcast(E4M3),
+                    lhsT_scale=w_scales[e][:, a * K : (a + 1) * K],
+                    rhs=slot_words[e][a].bitcast(E5M2),
+                    rhs_scale=slot_plane[a][:, e * C : (e + 1) * C],
+                    start=(a == 0),
+                    stop=(a == PASSES - 1),
+                )
+
+        def apply_gate(e):
+            g = gate_sb[e // 3][:, (e % 3) * C : (e % 3 + 1) * C]
+            if USE_POOL and e < E - 1:
+                nc.scalar.copy(sums[e], acc[e][:])
+                nc.gpsimd.tensor_tensor(dx[:, e * C : (e + 1) * C], sums[e], g, MULT)
+            else:
+                nc.vector.tensor_tensor(dx[:, e * C : (e + 1) * C], acc[e][:], g, MULT)
+
+        for e in range(3):
+            gather_words(e, 0)
+        for lo in range(0, SLOTS, SCALE_PIECE):
+            nc.vector.tensor_copy(gathered_scales[:, lo : lo + SCALE_PIECE], packed[:].indirect(offs_sb[:, lo // 16 : (lo + SCALE_PIECE) // 16]))
+        for a in (1, 2):
+            shift(nc.gpsimd, slot_plane[a], gathered_scales, a)
+        for e in range(E + 1):
+            cast(e)
+        for e in range(3, E):
+            gather_words(e, 0)
+        for e in range(E):
+            quantise(e)
+            gather_words(e, 1)
+            if e >= 1 and not USE_POOL:
+                apply_gate(e - 1)
+            gather_words(e, 2)
+            multiply(e)
+            if USE_POOL and e < E - 1:
+                apply_gate(e)
+        quantise(E)
+        apply_gate(E - 1)
+        for h in range(2):
+            for a in range(PASSES):
+                nc.tensor.matmul_mx(
+                    out=acc_s[h][:],
+                    lhsT=w_codes[E][:, a * K : (a + 1) * K].bitcast(E4M3),
+                    lhsT_scale=w_scales[E][:, a * K : (a + 1) * K],
+                    rhs=words[a][:, h * C : (h + 1) * C].bitcast(E5M2),
+                    rhs_scale=tok_plane[a][:, h * C : (h + 1) * C],
+                    start=(a == 0),
+                    stop=(a == PASSES - 1),
+                )
+            nc.scalar.copy(ds[:, h * C : (h + 1) * C], acc_s[h][:])
+
+        for i, (lo, hi) in enumerate(PIECES):
+            total = ds[:, lo:hi]
+            picked = []
+            for r in range(3):
+                pick = keep.tile([P, hi - lo], F32, name="pick%d_%d" % (i, r))
+                nc.vector.tensor_copy(pick[:], dx[:].indirect(pos_sb[r][:, lo // 16 : hi // 16]))
+                picked.append(pick)
+                if USE_POOL:
+                    part = keep.tile([P, hi - lo], F32, name="part%d_%d" % (i, r))
+                    eng = nc.vector if (i == len(PIECES) - 1 and r == 2) else nc.gpsimd
+                    eng.tensor_tensor(part[:], total, pick[:], ADD)
+                    total = part[:]
+            if not USE_POOL:
+                for r in range(3):
+                    part = keep.tile([P, hi - lo], F32, name="part%d_%d" % (i, r))
+                    nc.vector.tensor_tensor(part[:], total, picked[r][:], ADD)
+                    total = part[:]
+            nc.sync.dma_start(out[:, lo:hi], total)

@@ -1,6 +1,7 @@
 from contextlib import ExitStack
 
 import concourse.mybir as mybir
+from concourse.masks import make_identity
 
 K, T, E, C, N = 128, 1024, 6, 512, 1536
 P = 128
@@ -20,10 +21,13 @@ E5M2 = mybir.dt.float8_e5m2_x4
 MULT = mybir.AluOpType.mult
 ADD = mybir.AluOpType.add
 
-USE_POOL = True
-SHIFT_ROWS = 112
+COPY = mybir.ActivationFunctionType.Copy
+TURNED = 3
+EARLY = 4
+GATE_BLOCKS = 16
+BLOCKS = 4
+PLANE_AT = {1: (8, 112), 2: (28, 100)}
 SCALE_PIECE = 768
-PIECES = [(0, 512), (512, 1024)]
 
 
 def tile_moe_bds_lin_none_kernel(tc, dy_words, dy_scales, w, gate, offs, pos1, pos2, pos3, out):
@@ -34,6 +38,9 @@ def tile_moe_bds_lin_none_kernel(tc, dy_words, dy_scales, w, gate, offs, pos1, p
         reuse = ctx.enter_context(tc.tile_pool(name="reuse", bufs=1))
         psum = ctx.enter_context(tc.psum_pool(name="psum", bufs=1))
 
+        def bank(i, name):
+            return psum.tile([P, C], F32, name=name, tag="bank%d" % i)
+
         offs_sb = lists.tile([P, SLOTS // 16], U16, name="offs_sb")
         pos_sb = [lists.tile([P, T // 16], U16, name="pos%d_sb" % r) for r in range(3)]
         words = [keep.tile([P, T], I32, name="words%d" % a, align_bytes=64) for a in range(PASSES)]
@@ -42,53 +49,68 @@ def tile_moe_bds_lin_none_kernel(tc, dy_words, dy_scales, w, gate, offs, pos1, p
         gathered_scales = keep.tile([P, SLOTS], U8, name="gathered_scales", align_bytes=64)
         slot_plane = [gathered_scales] + [keep.tile([P, SLOTS], U8, name="slot_plane%d" % a, align_bytes=64) for a in (1, 2)]
         raw_bytes = PASSES * PACK * K * 4
-        w_raw = [reuse.tile([P, PASSES, PACK, K], F32, name="w_raw%d" % e, align_bytes=64, offset=e * raw_bytes) for e in range(E + 1)]
-        first = [keep.tile([P, C], U32, name="slot_first%d" % e, align_bytes=64) for e in range(E)]
-        rest = [reuse.tile([P, 2, C], U32, name="slot_rest%d" % e, align_bytes=64, offset=e * raw_bytes) for e in range(E)]
-        slot_words = [[first[e][:], rest[e][:, 0, :], rest[e][:, 1, :]] for e in range(E)]
+        raw_at = [e * raw_bytes for e in range(E - 1)] + [(E + 1) * raw_bytes, (E - 1) * raw_bytes]
+        last_raw = raw_at[E - 1]
+        spare = last_raw + raw_bytes + 256
+        w_raw = [reuse.tile([P, PASSES, PACK, K], F32, name="w_raw%d" % e, align_bytes=64, offset=raw_at[e]) for e in range(E + 1)]
+        slot_words = []
+        for e in range(E):
+            if e < EARLY:
+                first = keep.tile([P, C], U32, name="slot_first%d" % e, align_bytes=64)
+                rest = reuse.tile([P, 2, C], U32, name="slot_rest%d" % e, align_bytes=64, offset=raw_at[e])
+                slot_words.append([first[:], rest[:, 0, :], rest[:, 1, :]])
+            else:
+                at = raw_at[e] if e < E - 1 else last_raw - raw_bytes + 64
+                rest = reuse.tile([P, PASSES, C], U32, name="slot_rest%d" % e, align_bytes=64, offset=at)
+                slot_words.append([rest[:, a, :] for a in range(PASSES)])
         w_bf = [keep.tile([P, PASSES * K * PACK], BF16, name="w_bf%d" % e, align_bytes=64) for e in range(E + 1)]
-        w_codes = [keep.tile([P, PASSES * K], U32, name="w_codes%d" % e, align_bytes=64) for e in range(E)]
-        w_codes.append(reuse.tile([P, PASSES * K], U32, name="w_codes_shared", align_bytes=64, offset=(E - 1) * raw_bytes + 2 * C * 4))
+        w_codes = [keep.tile([P, PASSES * K], U32, name="w_codes%d" % e, align_bytes=64) for e in range(E + 1)]
         w_scales = [keep.tile([P, PASSES * K], U8, name="w_scales%d" % e, align_bytes=64) for e in range(E + 1)]
-        gate_sb = [keep.tile([P, SLOTS // 2], F32, name="gate%d" % h) for h in range(2)]
-        sums_all = reuse.tile([P, E - 1, C], F32, name="sums_all", align_bytes=64, offset=E * raw_bytes)
-        sums = [sums_all[:, e, :] for e in range(E - 1)]
+        gate_last = keep.tile([P, (E - TURNED) * C], F32, name="gate_last")
+        gate_rows = keep.tile([P, P], F32, name="gate_rows")
+        gate_cols = keep.tile([P, TURNED * BLOCKS], F32, name="gate_cols")
+        ident = keep.tile([P, P], F32, name="ident")
         dx = keep.tile([P, SLOTS], F32, name="dx")
-        ds = keep.tile([P, T], F32, name="ds")
-        acc = [psum.tile([P, C], F32, name="acc%d" % e) for e in range(E)]
-        acc_s = [psum.tile([P, C], F32, name="acc_s%d" % h) for h in range(2)]
+        ds = reuse.tile([P, T], F32, name="ds", align_bytes=64, offset=last_raw + 64 + C * 4)
 
-        nc.gpsimd.memset(packed[:].bitcast(I32), 0)
         nc.sync.dma_start(offs_sb[:], offs)
-        for a in range(PASSES):
+
+        def load_words(a):
             nc.sync.dma_start(words[a][:], dy_words[a].rearrange("p t d -> p (t d)").bitcast(I32))
-        for q in range(4):
-            nc.scalar.dma_start(packed[32 * q : 32 * q + 12, :].bitcast(I32), dy_scales[:, 4 * q : 4 * q + 4, :].bitcast(I32))
-        for a in (1, 2):
-            nc.gpsimd.memset(slot_plane[a][:].bitcast(I32), 0)
-            nc.gpsimd.memset(tok_plane[a][:].bitcast(I32), 0)
 
         def load_w(e):
             nc.sync.dma_start(w_raw[e][:], w[e].rearrange("(a p j) k -> p a j k", a=PASSES, j=PACK))
 
-        def load_gate(h):
-            nc.sync.dma_start(gate_sb[h][:], gate[:, h * (SLOTS // 2) : (h + 1) * (SLOTS // 2)])
-
-        for e in range(E + 1):
-            load_w(e)
-        load_gate(0)
-        load_gate(1)
-        for r, pos in enumerate((pos1, pos2, pos3)):
-            nc.sync.dma_start(pos_sb[r][:], pos)
+        load_words(0)
+        scale_rows = dy_scales.rearrange("a f t -> (a f) t").bitcast(I32)
+        for q in range(4):
+            for half in range(2):
+                rows = scale_rows[4 * (q + half) : 4 * (q + half) + 32, :].rearrange("(g f) t -> g f t", g=2)
+                nc.sync.dma_start(packed[32 * q + 16 * half : 32 * q + 16 * half + 16, :].bitcast(I32), rows[:, 8 * half : 8 * half + 8, :])
+        for a in (1, 2):
+            nc.vector.memset(tok_plane[a][:].bitcast(I32), 0)
+            nc.vector.memset(slot_plane[a][:].bitcast(I32), 0)
+        make_identity(nc, ident[:])
 
         def shift(queue, dst, src, a):
-            queue.dma_start(dst[0:SHIFT_ROWS, :].bitcast(I32), src[4 * a : 4 * a + SHIFT_ROWS, :].bitcast(I32))
+            first, rows = PLANE_AT[a]
+            queue.dma_start(dst[0:rows, :].bitcast(I32), src[first : first + rows, :].bitcast(I32))
 
         for a in (1, 2):
             shift(nc.gpsimd, tok_plane[a], packed, a)
+        nc.sync.dma_start(gate_rows[:], gate[0 : P // GATE_BLOCKS, 0 : GATE_BLOCKS * P].rearrange("r (c p) -> r c p", p=P))
+        load_w(E)
+        load_w(0)
+        load_words(1)
+        load_words(2)
+        for e in range(1, E):
+            load_w(e)
+        nc.sync.dma_start(gate_last[:], gate[:, TURNED * C :])
+        for r, pos in enumerate((pos1, pos2, pos3)):
+            nc.sync.dma_start(pos_sb[r][:], pos)
 
         def cast(e):
-            nc.scalar.copy(w_bf[e][:].rearrange("p (a k j) -> p a k j", a=PASSES, j=PACK), w_raw[e][:].rearrange("p a j k -> p a k j"))
+            nc.scalar.copy(w_bf[e][:].rearrange("p (a c i j) -> p a c j i", a=PASSES, i=4, j=PACK), w_raw[e][:].rearrange("p a j (c i) -> p a c j i", i=4))
 
         def quantise(e):
             for lo, hi in ((0, 2 * K), (2 * K, 3 * K)):
@@ -97,75 +119,100 @@ def tile_moe_bds_lin_none_kernel(tc, dy_words, dy_scales, w, gate, offs, pos1, p
         def gather_words(e, a):
             nc.vector.tensor_copy(slot_words[e][a], words[a][:].bitcast(U32).indirect(offs_sb[:, e * C // 16 : (e + 1) * C // 16]))
 
-        def multiply(e):
+        def multiply(acc, e, moving, planes):
             for a in range(PASSES):
                 nc.tensor.matmul_mx(
-                    out=acc[e][:],
+                    out=acc[:],
                     lhsT=w_codes[e][:, a * K : (a + 1) * K].bitcast(E4M3),
                     lhsT_scale=w_scales[e][:, a * K : (a + 1) * K],
-                    rhs=slot_words[e][a].bitcast(E5M2),
-                    rhs_scale=slot_plane[a][:, e * C : (e + 1) * C],
+                    rhs=moving[a].bitcast(E5M2),
+                    rhs_scale=planes[a],
                     start=(a == 0),
                     stop=(a == PASSES - 1),
                 )
 
-        def apply_gate(e):
-            g = gate_sb[e // 3][:, (e % 3) * C : (e % 3 + 1) * C]
-            if USE_POOL and e < E - 1:
-                nc.scalar.copy(sums[e], acc[e][:])
-                nc.gpsimd.tensor_tensor(dx[:, e * C : (e + 1) * C], sums[e], g, MULT)
-            else:
-                nc.vector.tensor_tensor(dx[:, e * C : (e + 1) * C], acc[e][:], g, MULT)
+        def block(b):
+            return slice(b * P, (b + 1) * P)
 
-        for e in range(3):
+        def gate_by_turning(e, acc):
+            sums = reuse.tile([P, C], F32, name="sums%d" % e, align_bytes=64, offset=last_raw + 64)
+            nc.scalar.copy(sums[:], acc[:])
+            turned = bank(3, "turned%d" % e)
+            for b in range(BLOCKS):
+                nc.tensor.transpose(turned[:, block(b)], sums[:, block(b)], ident[:])
+            scaled = keep.tile([P, C], F32, name="scaled%d" % e)
+            for b in range(BLOCKS):
+                col = e * BLOCKS + b
+                nc.scalar.activation(scaled[:, block(b)], turned[:, block(b)], COPY, scale=gate_cols[:, col : col + 1])
+            back = bank(4, "back%d" % e)
+            for b in range(BLOCKS):
+                nc.tensor.transpose(back[:, block(b)], scaled[:, block(b)], ident[:])
+            nc.scalar.copy(dx[:, e * C : (e + 1) * C], back[:])
+
+        for e in range(EARLY):
             gather_words(e, 0)
         for lo in range(0, SLOTS, SCALE_PIECE):
             nc.vector.tensor_copy(gathered_scales[:, lo : lo + SCALE_PIECE], packed[:].indirect(offs_sb[:, lo // 16 : (lo + SCALE_PIECE) // 16]))
         for a in (1, 2):
             shift(nc.gpsimd, slot_plane[a], gathered_scales, a)
-        for e in range(E + 1):
+        gate_turned = bank(3, "gate_turned")
+        nc.tensor.transpose(gate_turned[:, 0:P], gate_rows[:], ident[:])
+        nc.scalar.copy(gate_cols[:], gate_turned[:, 0 : TURNED * BLOCKS])
+        for e in [E] + list(range(E)):
             cast(e)
-        for e in range(3, E):
-            gather_words(e, 0)
+        quantise(E)
+        shared = []
+        for h in range(2):
+            cols = slice(h * C, (h + 1) * C)
+            acc = bank(6 + h, "acc_shared%d" % h)
+            multiply(acc, E, [words[a][:, cols] for a in range(PASSES)], [tok_plane[a][:, cols] for a in range(PASSES)])
+            shared.append(acc)
+        late = []
         for e in range(E):
             quantise(e)
-            gather_words(e, 1)
-            if e >= 1 and not USE_POOL:
-                apply_gate(e - 1)
-            gather_words(e, 2)
-            multiply(e)
-            if USE_POOL and e < E - 1:
-                apply_gate(e)
-        quantise(E)
-        apply_gate(E - 1)
+            for a in range(1 if e < EARLY else 0, PASSES):
+                gather_words(e, a)
+            acc = bank((0, 1, 0, 0, 3, 4)[e], "acc%d" % e)
+            multiply(acc, e, slot_words[e], [slot_plane[a][:, e * C : (e + 1) * C] for a in range(PASSES)])
+            if e < TURNED:
+                gate_by_turning(e, acc)
+            else:
+                late.append((e, acc))
         for h in range(2):
-            for a in range(PASSES):
-                nc.tensor.matmul_mx(
-                    out=acc_s[h][:],
-                    lhsT=w_codes[E][:, a * K : (a + 1) * K].bitcast(E4M3),
-                    lhsT_scale=w_scales[E][:, a * K : (a + 1) * K],
-                    rhs=words[a][:, h * C : (h + 1) * C].bitcast(E5M2),
-                    rhs_scale=tok_plane[a][:, h * C : (h + 1) * C],
-                    start=(a == 0),
-                    stop=(a == PASSES - 1),
-                )
-            nc.scalar.copy(ds[:, h * C : (h + 1) * C], acc_s[h][:])
+            nc.scalar.copy(ds[:, h * C : (h + 1) * C], shared[h][:])
+        for e, acc in late:
+            nc.vector.tensor_tensor(dx[:, e * C : (e + 1) * C], acc[:], gate_last[:, (e - TURNED) * C : (e - TURNED + 1) * C], MULT)
 
-        for i, (lo, hi) in enumerate(PIECES):
-            total = ds[:, lo:hi]
-            picked = []
-            for r in range(3):
-                pick = keep.tile([P, hi - lo], F32, name="pick%d_%d" % (i, r))
-                nc.vector.tensor_copy(pick[:], dx[:].indirect(pos_sb[r][:, lo // 16 : hi // 16]))
-                picked.append(pick)
-                if USE_POOL:
-                    part = keep.tile([P, hi - lo], F32, name="part%d_%d" % (i, r))
-                    eng = nc.vector if (i == len(PIECES) - 1 and r == 2) else nc.gpsimd
-                    eng.tensor_tensor(part[:], total, pick[:], ADD)
-                    total = part[:]
-            if not USE_POOL:
-                for r in range(3):
-                    part = keep.tile([P, hi - lo], F32, name="part%d_%d" % (i, r))
-                    nc.vector.tensor_tensor(part[:], total, picked[r][:], ADD)
-                    total = part[:]
-            nc.sync.dma_start(out[:, lo:hi], total)
+        def pick(h, r, offset=None):
+            if offset is None:
+                t = keep.tile([P, C], F32, name="pick%d_%d" % (h, r))
+            else:
+                t = reuse.tile([P, C], F32, name="pick%d_%d" % (h, r), align_bytes=64, offset=offset)
+            nc.vector.tensor_copy(t[:], dx[:].indirect(pos_sb[r][:, h * C // 16 : (h + 1) * C // 16]))
+            return t
+
+        def partial_sum(h, terms, offset):
+            turned = bank(2 - h, "sum%d" % h)
+            for n, term in enumerate(terms):
+                for b in range(BLOCKS):
+                    nc.tensor.matmul(turned[:, block(b)], term[:, block(b)], ident[:], start=(n == 0 and b == 0), stop=(n == len(terms) - 1 and b == BLOCKS - 1), is_transpose=True)
+            staged = reuse.tile([P, C], F32, name="staged%d" % h, align_bytes=64, offset=offset)
+            nc.scalar.copy(staged[:], turned[:])
+            back = bank(5 + h, "sum_back%d" % h)
+            for b in range(BLOCKS):
+                nc.tensor.transpose(back[:, block(b)], staged[:, block(b)], ident[:])
+            return back
+
+        def finish(h, back, last):
+            total = keep.tile([P, C], F32, name="total%d" % h)
+            nc.vector.tensor_tensor(total[:], back[:], last[:], ADD)
+            nc.sync.dma_start(out[:, h * C : (h + 1) * C], total[:])
+
+        p00 = pick(0, 0)
+        p01 = pick(0, 1)
+        back0 = partial_sum(0, [ds[:, 0:C], p00[:], p01[:]], spare)
+        p10 = pick(1, 0)
+        p11 = pick(1, 1)
+        back1 = partial_sum(1, [ds[:, C:T], p10[:], p11[:]], spare + C * 4)
+        finish(0, back0, pick(0, 2))
+        finish(1, back1, pick(1, 2, spare))

@@ -21,10 +21,8 @@ E5M2 = mybir.dt.float8_e5m2_x4
 MULT = mybir.AluOpType.mult
 ADD = mybir.AluOpType.add
 
-COPY = mybir.ActivationFunctionType.Copy
-TURNED = 3
+POOLED = 4
 EARLY = 4
-GATE_BLOCKS = 16
 BLOCKS = 4
 PLANE_AT = {1: (8, 112), 2: (28, 100)}
 SCALE_PIECE = 768
@@ -51,7 +49,6 @@ def tile_moe_bds_lin_none_kernel(tc, dy_words, dy_scales, w, gate, offs, pos1, p
         raw_bytes = PASSES * PACK * K * 4
         raw_at = [e * raw_bytes for e in range(E - 1)] + [(E + 1) * raw_bytes, (E - 1) * raw_bytes]
         last_raw = raw_at[E - 1]
-        spare = last_raw + raw_bytes + 256
         w_raw = [reuse.tile([P, PASSES, PACK, K], F32, name="w_raw%d" % e, align_bytes=64, offset=raw_at[e]) for e in range(E + 1)]
         slot_words = []
         for e in range(E):
@@ -66,12 +63,12 @@ def tile_moe_bds_lin_none_kernel(tc, dy_words, dy_scales, w, gate, offs, pos1, p
         w_bf = [keep.tile([P, PASSES * K * PACK], BF16, name="w_bf%d" % e, align_bytes=64) for e in range(E + 1)]
         w_codes = [keep.tile([P, PASSES * K], U32, name="w_codes%d" % e, align_bytes=64) for e in range(E + 1)]
         w_scales = [keep.tile([P, PASSES * K], U8, name="w_scales%d" % e, align_bytes=64) for e in range(E + 1)]
-        gate_last = keep.tile([P, (E - TURNED) * C], F32, name="gate_last")
-        gate_rows = keep.tile([P, P], F32, name="gate_rows")
-        gate_cols = keep.tile([P, TURNED * BLOCKS], F32, name="gate_cols")
+        gate_first = keep.tile([P, POOLED * C], F32, name="gate_first")
+        gate_last = keep.tile([P, (E - POOLED) * C], F32, name="gate_last")
         ident = keep.tile([P, P], F32, name="ident")
         dx = keep.tile([P, SLOTS], F32, name="dx")
-        ds = reuse.tile([P, T], F32, name="ds", align_bytes=64, offset=last_raw + 64 + C * 4)
+        ds = reuse.tile([P, T], F32, name="ds", align_bytes=64, offset=last_raw + 64)
+        sums = reuse.tile([P, POOLED, C], F32, name="sums", align_bytes=64, offset=last_raw + 64 + T * 4)
 
         nc.sync.dma_start(offs_sb[:], offs)
 
@@ -98,14 +95,14 @@ def tile_moe_bds_lin_none_kernel(tc, dy_words, dy_scales, w, gate, offs, pos1, p
 
         for a in (1, 2):
             shift(nc.gpsimd, tok_plane[a], packed, a)
-        nc.sync.dma_start(gate_rows[:], gate[0 : P // GATE_BLOCKS, 0 : GATE_BLOCKS * P].rearrange("r (c p) -> r c p", p=P))
         load_w(E)
         load_w(0)
         load_words(1)
         load_words(2)
         for e in range(1, E):
             load_w(e)
-        nc.sync.dma_start(gate_last[:], gate[:, TURNED * C :])
+        nc.sync.dma_start(gate_first[:], gate[:, 0 : POOLED * C])
+        nc.sync.dma_start(gate_last[:], gate[:, POOLED * C :])
         for r, pos in enumerate((pos1, pos2, pos3)):
             nc.sync.dma_start(pos_sb[r][:], pos)
 
@@ -134,30 +131,12 @@ def tile_moe_bds_lin_none_kernel(tc, dy_words, dy_scales, w, gate, offs, pos1, p
         def block(b):
             return slice(b * P, (b + 1) * P)
 
-        def gate_by_turning(e, acc):
-            sums = reuse.tile([P, C], F32, name="sums%d" % e, align_bytes=64, offset=last_raw + 64)
-            nc.scalar.copy(sums[:], acc[:])
-            turned = bank(3, "turned%d" % e)
-            for b in range(BLOCKS):
-                nc.tensor.transpose(turned[:, block(b)], sums[:, block(b)], ident[:])
-            scaled = keep.tile([P, C], F32, name="scaled%d" % e)
-            for b in range(BLOCKS):
-                col = e * BLOCKS + b
-                nc.scalar.activation(scaled[:, block(b)], turned[:, block(b)], COPY, scale=gate_cols[:, col : col + 1])
-            back = bank(4, "back%d" % e)
-            for b in range(BLOCKS):
-                nc.tensor.transpose(back[:, block(b)], scaled[:, block(b)], ident[:])
-            nc.scalar.copy(dx[:, e * C : (e + 1) * C], back[:])
-
         for e in range(EARLY):
             gather_words(e, 0)
         for lo in range(0, SLOTS, SCALE_PIECE):
             nc.vector.tensor_copy(gathered_scales[:, lo : lo + SCALE_PIECE], packed[:].indirect(offs_sb[:, lo // 16 : (lo + SCALE_PIECE) // 16]))
         for a in (1, 2):
             shift(nc.gpsimd, slot_plane[a], gathered_scales, a)
-        gate_turned = bank(3, "gate_turned")
-        nc.tensor.transpose(gate_turned[:, 0:P], gate_rows[:], ident[:])
-        nc.scalar.copy(gate_cols[:], gate_turned[:, 0 : TURNED * BLOCKS])
         for e in [E] + list(range(E)):
             cast(e)
         quantise(E)
@@ -172,47 +151,49 @@ def tile_moe_bds_lin_none_kernel(tc, dy_words, dy_scales, w, gate, offs, pos1, p
             quantise(e)
             for a in range(1 if e < EARLY else 0, PASSES):
                 gather_words(e, a)
-            acc = bank((0, 1, 0, 0, 3, 4)[e], "acc%d" % e)
+            acc = bank(e % POOLED, "acc%d" % e)
             multiply(acc, e, slot_words[e], [slot_plane[a][:, e * C : (e + 1) * C] for a in range(PASSES)])
-            if e < TURNED:
-                gate_by_turning(e, acc)
+            if e < POOLED:
+                nc.scalar.copy(sums[:, e, :], acc[:])
+                nc.gpsimd.tensor_tensor(dx[:, e * C : (e + 1) * C], sums[:, e, :], gate_first[:, e * C : (e + 1) * C], MULT)
             else:
                 late.append((e, acc))
         for h in range(2):
             nc.scalar.copy(ds[:, h * C : (h + 1) * C], shared[h][:])
         for e, acc in late:
-            nc.vector.tensor_tensor(dx[:, e * C : (e + 1) * C], acc[:], gate_last[:, (e - TURNED) * C : (e - TURNED + 1) * C], MULT)
+            nc.vector.tensor_tensor(dx[:, e * C : (e + 1) * C], acc[:], gate_last[:, (e - POOLED) * C : (e - POOLED + 1) * C], MULT)
 
-        def pick(h, r, offset=None):
-            if offset is None:
-                t = keep.tile([P, C], F32, name="pick%d_%d" % (h, r))
-            else:
-                t = reuse.tile([P, C], F32, name="pick%d_%d" % (h, r), align_bytes=64, offset=offset)
+        def pick(h, r):
+            t = keep.tile([P, C], F32, name="pick%d_%d" % (h, r))
             nc.vector.tensor_copy(t[:], dx[:].indirect(pos_sb[r][:, h * C // 16 : (h + 1) * C // 16]))
             return t
 
-        def partial_sum(h, terms, offset):
-            turned = bank(2 - h, "sum%d" % h)
-            for n, term in enumerate(terms):
-                for b in range(BLOCKS):
-                    nc.tensor.matmul(turned[:, block(b)], term[:, block(b)], ident[:], start=(n == 0 and b == 0), stop=(n == len(terms) - 1 and b == BLOCKS - 1), is_transpose=True)
-            staged = reuse.tile([P, C], F32, name="staged%d" % h, align_bytes=64, offset=offset)
-            nc.scalar.copy(staged[:], turned[:])
-            back = bank(5 + h, "sum_back%d" % h)
+        turned = bank(4, "turned")
+
+        def turn(term, n):
             for b in range(BLOCKS):
-                nc.tensor.transpose(back[:, block(b)], staged[:, block(b)], ident[:])
-            return back
+                nc.tensor.matmul(turned[:, block(b)], term[:, block(b)], ident[:], start=(n == 0 and b == 0), stop=(n == 2 and b == BLOCKS - 1), is_transpose=True)
 
-        def finish(h, back, last):
-            total = keep.tile([P, C], F32, name="total%d" % h)
-            nc.vector.tensor_tensor(total[:], back[:], last[:], ADD)
-            nc.sync.dma_start(out[:, h * C : (h + 1) * C], total[:])
+        def pool_add(n, x, y):
+            t = keep.tile([P, C], F32, name="part%d" % n)
+            nc.gpsimd.tensor_tensor(t[:], x, y, ADD)
+            return t
 
-        p00 = pick(0, 0)
-        p01 = pick(0, 1)
-        back0 = partial_sum(0, [ds[:, 0:C], p00[:], p01[:]], spare)
-        p10 = pick(1, 0)
-        p11 = pick(1, 1)
-        back1 = partial_sum(1, [ds[:, C:T], p10[:], p11[:]], spare + C * 4)
-        finish(0, back0, pick(0, 2))
-        finish(1, back1, pick(1, 2, spare))
+        turn(ds[:, C:T], 0)
+        turn(pick(1, 0)[:], 1)
+        part = pool_add(0, ds[:, 0:C], pick(0, 0)[:])
+        turn(pick(1, 1)[:], 2)
+        staged = keep.tile([P, C], F32, name="staged")
+        nc.scalar.copy(staged[:], turned[:])
+        back = bank(5, "back")
+        for b in range(BLOCKS):
+            nc.tensor.transpose(back[:, block(b)], staged[:, block(b)], ident[:])
+        part = pool_add(1, part[:], pick(0, 1)[:])
+        part = pool_add(2, part[:], pick(0, 2)[:])
+        nc.sync.dma_start(out[:, 0:C], part[:])
+        last = pick(1, 2)
+        for i in range(2):
+            cols = slice(i * C // 2, (i + 1) * C // 2)
+            total = keep.tile([P, C // 2], F32, name="total%d" % i)
+            nc.vector.tensor_tensor(total[:], back[:, cols], last[:, cols], ADD)
+            nc.scalar.dma_start(out[:, C + i * C // 2 : C + (i + 1) * C // 2], total[:])

@@ -4,11 +4,26 @@ import concourse.mybir as mybir
 from concourse.masks import make_identity
 
 K, T, E, C, N = 128, 1024, 6, 512, 1536
-P = 128
-PACK = 4
-PASSES = 3
+SHARED = E
+LAST = E - 1
 SLOTS = E * C
 FLOPS = 2 * K * N * (SLOTS + T)
+
+P = 128
+PACK = 4
+PASSES = N // (P * PACK)
+PER_COLUMN = 16
+HALF = T // 2
+BLOCKS = HALF // P
+
+STACK_ROW = (0, 8, 28)
+MOVED_ROWS = (0, 112, 100)
+SCALE_PIECE = 768
+RUN = 4
+STAGGERED = 3
+
+WORDS_BYTES = C * 4
+RAW_BYTES = PASSES * PACK * K * 4
 
 F32 = mybir.dt.float32
 BF16 = mybir.dt.bfloat16
@@ -20,12 +35,6 @@ E4M3 = mybir.dt.float8_e4m3fn_x4
 E5M2 = mybir.dt.float8_e5m2_x4
 MULT = mybir.AluOpType.mult
 ADD = mybir.AluOpType.add
-
-POOLED = 4
-EARLY = 4
-BLOCKS = 4
-PLANE_AT = {1: (8, 112), 2: (28, 100)}
-SCALE_PIECE = 768
 
 
 def tile_moe_bds_lin_none_kernel(tc, dy_words, dy_scales, w, gate, offs, pos1, pos2, pos3, out):
@@ -39,38 +48,45 @@ def tile_moe_bds_lin_none_kernel(tc, dy_words, dy_scales, w, gate, offs, pos1, p
         def bank(i, name):
             return psum.tile([P, C], F32, name=name, tag="bank%d" % i)
 
-        offs_sb = lists.tile([P, SLOTS // 16], U16, name="offs_sb")
-        pos_sb = [lists.tile([P, T // 16], U16, name="pos%d_sb" % r) for r in range(3)]
-        words = [keep.tile([P, T], I32, name="words%d" % a, align_bytes=64) for a in range(PASSES)]
-        packed = keep.tile([P, T], U8, name="packed", align_bytes=64)
-        tok_plane = [packed] + [keep.tile([P, T], U8, name="tok_plane%d" % a, align_bytes=64) for a in (1, 2)]
-        gathered_scales = keep.tile([P, SLOTS], U8, name="gathered_scales", align_bytes=64)
-        slot_plane = [gathered_scales] + [keep.tile([P, SLOTS], U8, name="slot_plane%d" % a, align_bytes=64) for a in (1, 2)]
-        raw_bytes = PASSES * PACK * K * 4
-        raw_at = [e * raw_bytes for e in range(E - 1)] + [(E + 1) * raw_bytes, (E - 1) * raw_bytes]
-        last_raw = raw_at[E - 1]
-        w_raw = [reuse.tile([P, PASSES, PACK, K], F32, name="w_raw%d" % e, align_bytes=64, offset=raw_at[e]) for e in range(E + 1)]
-        slot_words = []
-        for e in range(E):
-            if e < EARLY:
-                first = keep.tile([P, C], U32, name="slot_first%d" % e, align_bytes=64)
-                rest = reuse.tile([P, 2, C], U32, name="slot_rest%d" % e, align_bytes=64, offset=raw_at[e])
-                slot_words.append([first[:], rest[:, 0, :], rest[:, 1, :]])
-            else:
-                at = raw_at[e] if e < E - 1 else last_raw - raw_bytes + 64
-                rest = reuse.tile([P, PASSES, C], U32, name="slot_rest%d" % e, align_bytes=64, offset=at)
-                slot_words.append([rest[:, a, :] for a in range(PASSES)])
-        w_bf = [keep.tile([P, PASSES * K * PACK], BF16, name="w_bf%d" % e, align_bytes=64) for e in range(E + 1)]
-        w_codes = [keep.tile([P, PASSES * K], U32, name="w_codes%d" % e, align_bytes=64) for e in range(E + 1)]
-        w_scales = [keep.tile([P, PASSES * K], U8, name="w_scales%d" % e, align_bytes=64) for e in range(E + 1)]
-        gate_first = keep.tile([P, POOLED * C], F32, name="gate_first")
-        gate_last = keep.tile([P, (E - POOLED) * C], F32, name="gate_last")
-        ident = keep.tile([P, P], F32, name="ident")
-        dx = keep.tile([P, SLOTS], F32, name="dx")
-        ds = reuse.tile([P, T], F32, name="ds", align_bytes=64, offset=last_raw + 64)
-        sums = reuse.tile([P, POOLED, C], F32, name="sums", align_bytes=64, offset=last_raw + 64 + T * 4)
+        def kept(shape, dtype, name):
+            return keep.tile(shape, dtype, name=name, align_bytes=64)
 
-        nc.sync.dma_start(offs_sb[:], offs)
+        def placed(shape, dtype, name, offset):
+            return reuse.tile(shape, dtype, name=name, align_bytes=64, offset=offset)
+
+        offs_sb = lists.tile([P, SLOTS // PER_COLUMN], U16, name="offs_sb")
+        pos_sb = [lists.tile([P, T // PER_COLUMN], U16, name="pos%d_sb" % r) for r in range(3)]
+
+        words = [kept([P, T], I32, "words%d" % a) for a in range(PASSES)]
+        token_stack = kept([P, T], U8, "token_stack")
+        slot_stack = kept([P, SLOTS], U8, "slot_stack")
+        token_plane = [token_stack] + [kept([P, T], U8, "token_plane%d" % a) for a in range(1, PASSES)]
+        slot_plane = [slot_stack] + [kept([P, SLOTS], U8, "slot_plane%d" % a) for a in range(1, PASSES)]
+
+        raw_at = [e * RAW_BYTES for e in range(LAST)] + [E * RAW_BYTES, LAST * RAW_BYTES]
+        w_raw = [placed([P, PASSES, PACK, K], F32, "w_raw%d" % e, raw_at[e]) for e in range(E + 1)]
+        first_pass = [kept([P, C], U32, "first_pass%d" % e) for e in range(LAST - 1)]
+        first_pass.append(placed([P, C], U32, "first_pass_4", raw_at[0] + 2 * WORDS_BYTES))
+        first_pass.append(placed([P, C], U32, "first_pass_last", raw_at[LAST]))
+        later = [placed([P, 2, C], U32, "later%d" % e, raw_at[e])[:] for e in range(STAGGERED)]
+        late_at = raw_at[LAST] + WORDS_BYTES
+        late = placed([P, E - STAGGERED, 2, C], U32, "late", late_at)
+        later += [late[:, e, :, :] for e in range(E - STAGGERED)]
+        slot_words = [[first_pass[e][:], later[e][:, 0, :], later[e][:, 1, :]] for e in range(E)]
+
+        drained_at = late_at + (E - STAGGERED) * 2 * WORDS_BYTES
+        w_bf = [kept([P, PASSES * K * PACK], BF16, "w_bf%d" % e) for e in range(LAST)]
+        w_bf.append(placed([P, PASSES * K * PACK], BF16, "w_bf_last", drained_at))
+        w_bf.append(kept([P, PASSES * K * PACK], BF16, "w_bf_shared"))
+        drained = placed([P, LAST + 2, C], F32, "drained", drained_at)
+        ds = [drained[:, LAST + h, :] for h in range(2)]
+        w_codes = [kept([P, PASSES * K], U32, "w_codes%d" % e) for e in range(E)]
+        w_codes.append(placed([P, PASSES * K], U32, "w_codes_shared", raw_at[LAST]))
+        w_scales = [kept([P, PASSES * K], U8, "w_scales%d" % e) for e in range(E + 1)]
+
+        gate_sb = kept([P, SLOTS], F32, "gate_sb")
+        ident = kept([P, P], F32, "ident")
+        dx = kept([P, SLOTS], F32, "dx")
 
         def load_words(a):
             nc.sync.dma_start(words[a][:], dy_words[a].rearrange("p t d -> p (t d)").bitcast(I32))
@@ -78,43 +94,48 @@ def tile_moe_bds_lin_none_kernel(tc, dy_words, dy_scales, w, gate, offs, pos1, p
         def load_w(e):
             nc.sync.dma_start(w_raw[e][:], w[e].rearrange("(a p j) k -> p a j k", a=PASSES, j=PACK))
 
+        def move_plane(plane, stack, a):
+            rows = MOVED_ROWS[a]
+            nc.gpsimd.dma_start(plane[0:rows, :].bitcast(I32), stack[STACK_ROW[a] : STACK_ROW[a] + rows, :].bitcast(I32))
+
+        nc.sync.dma_start(offs_sb[:], offs)
         load_words(0)
         scale_rows = dy_scales.rearrange("a f t -> (a f) t").bitcast(I32)
         for q in range(4):
-            for half in range(2):
-                rows = scale_rows[4 * (q + half) : 4 * (q + half) + 32, :].rearrange("(g f) t -> g f t", g=2)
-                nc.sync.dma_start(packed[32 * q + 16 * half : 32 * q + 16 * half + 16, :].bitcast(I32), rows[:, 8 * half : 8 * half + 8, :])
-        for a in (1, 2):
-            nc.vector.memset(tok_plane[a][:].bitcast(I32), 0)
+            for upper in range(2):
+                rows = scale_rows[4 * (q + upper) : 4 * (q + upper) + 32, :].rearrange("(g f) t -> g f t", g=2)
+                first = 32 * q + 16 * upper
+                nc.sync.dma_start(token_stack[first : first + 16, :].bitcast(I32), rows[:, 8 * upper : 8 * upper + 8, :])
+        for a in range(1, PASSES):
+            nc.vector.memset(token_plane[a][:].bitcast(I32), 0)
             nc.vector.memset(slot_plane[a][:].bitcast(I32), 0)
         make_identity(nc, ident[:])
-
-        def shift(queue, dst, src, a):
-            first, rows = PLANE_AT[a]
-            queue.dma_start(dst[0:rows, :].bitcast(I32), src[first : first + rows, :].bitcast(I32))
-
-        for a in (1, 2):
-            shift(nc.gpsimd, tok_plane[a], packed, a)
-        load_w(E)
+        for a in range(1, PASSES):
+            move_plane(token_plane[a], token_stack, a)
         load_w(0)
         load_words(1)
         load_words(2)
-        for e in range(1, E):
+        for e in range(1, E + 1):
             load_w(e)
-        nc.sync.dma_start(gate_first[:], gate[:, 0 : POOLED * C])
-        nc.sync.dma_start(gate_last[:], gate[:, POOLED * C :])
+        nc.sync.dma_start(gate_sb[:], gate)
         for r, pos in enumerate((pos1, pos2, pos3)):
             nc.sync.dma_start(pos_sb[r][:], pos)
 
-        def cast(e):
-            nc.scalar.copy(w_bf[e][:].rearrange("p (a c i j) -> p a c j i", a=PASSES, i=4, j=PACK), w_raw[e][:].rearrange("p a j (c i) -> p a c j i", i=4))
+        def round_w(e):
+            nc.scalar.copy(
+                w_bf[e][:].rearrange("p (a c i j) -> p a c j i", a=PASSES, i=RUN, j=PACK),
+                w_raw[e][:].rearrange("p a j (c i) -> p a c j i", i=RUN),
+            )
 
         def quantise(e):
-            for lo, hi in ((0, 2 * K), (2 * K, 3 * K)):
+            for lo, hi in ((0, 2 * K), (2 * K, PASSES * K)):
                 nc.vector.quantize_mx(out=w_codes[e][:, lo:hi].bitcast(E4M3), scales=w_scales[e][:, lo:hi], in_=w_bf[e][:, PACK * lo : PACK * hi])
 
+        def entries(list_sb, lo, hi):
+            return list_sb[:, lo // PER_COLUMN : hi // PER_COLUMN]
+
         def gather_words(e, a):
-            nc.vector.tensor_copy(slot_words[e][a], words[a][:].bitcast(U32).indirect(offs_sb[:, e * C // 16 : (e + 1) * C // 16]))
+            nc.vector.tensor_copy(slot_words[e][a], words[a][:].bitcast(U32).indirect(entries(offs_sb, e * C, (e + 1) * C)))
 
         def multiply(acc, e, moving, planes):
             for a in range(PASSES):
@@ -128,72 +149,75 @@ def tile_moe_bds_lin_none_kernel(tc, dy_words, dy_scales, w, gate, offs, pos1, p
                     stop=(a == PASSES - 1),
                 )
 
+        for e in range(LAST - 1):
+            gather_words(e, 0)
+        for lo in range(0, SLOTS, SCALE_PIECE):
+            nc.vector.tensor_copy(slot_stack[:, lo : lo + SCALE_PIECE], token_stack[:].indirect(entries(offs_sb, lo, lo + SCALE_PIECE)))
+        for a in range(1, PASSES):
+            move_plane(slot_plane[a], slot_stack, a)
+        for e in range(E + 1):
+            round_w(e)
+        gather_words(LAST - 1, 0)
+
+        for e in range(E):
+            slots = slice(e * C, (e + 1) * C)
+            if e < STAGGERED:
+                quantise(e)
+            elif e == STAGGERED:
+                for other in range(STAGGERED, E):
+                    quantise(other)
+            for a in range(0 if e == LAST else 1, PASSES):
+                gather_words(e, a)
+            acc = bank(e, "acc%d" % e)
+            multiply(acc, e, slot_words[e], [slot_plane[a][:, slots] for a in range(PASSES)])
+            if e < LAST:
+                nc.scalar.copy(drained[:, e, :], acc[:])
+                nc.gpsimd.tensor_tensor(dx[:, slots], drained[:, e, :], gate_sb[:, slots], MULT)
+            else:
+                quantise(SHARED)
+                nc.vector.tensor_tensor(dx[:, slots], acc[:], gate_sb[:, slots], MULT)
+
+        for h in (1, 0):
+            tokens = slice(h * HALF, (h + 1) * HALF)
+            acc = bank(E + h, "acc_shared%d" % h)
+            multiply(acc, SHARED, [words[a][:, tokens] for a in range(PASSES)], [token_plane[a][:, tokens] for a in range(PASSES)])
+            nc.scalar.copy(ds[h], acc[:])
+
+        def pick(h, r):
+            picked = kept([P, HALF], F32, "pick%d_%d" % (h, r))
+            nc.vector.tensor_copy(picked[:], dx[:].indirect(entries(pos_sb[r], h * HALF, (h + 1) * HALF)))
+            return picked[:]
+
         def block(b):
             return slice(b * P, (b + 1) * P)
 
-        for e in range(EARLY):
-            gather_words(e, 0)
-        for lo in range(0, SLOTS, SCALE_PIECE):
-            nc.vector.tensor_copy(gathered_scales[:, lo : lo + SCALE_PIECE], packed[:].indirect(offs_sb[:, lo // 16 : (lo + SCALE_PIECE) // 16]))
-        for a in (1, 2):
-            shift(nc.gpsimd, slot_plane[a], gathered_scales, a)
-        for e in [E] + list(range(E)):
-            cast(e)
-        quantise(E)
-        shared = []
-        for h in range(2):
-            cols = slice(h * C, (h + 1) * C)
-            acc = bank(6 + h, "acc_shared%d" % h)
-            multiply(acc, E, [words[a][:, cols] for a in range(PASSES)], [tok_plane[a][:, cols] for a in range(PASSES)])
-            shared.append(acc)
-        late = []
-        for e in range(E):
-            quantise(e)
-            for a in range(1 if e < EARLY else 0, PASSES):
-                gather_words(e, a)
-            acc = bank(e % POOLED, "acc%d" % e)
-            multiply(acc, e, slot_words[e], [slot_plane[a][:, e * C : (e + 1) * C] for a in range(PASSES)])
-            if e < POOLED:
-                nc.scalar.copy(sums[:, e, :], acc[:])
-                nc.gpsimd.tensor_tensor(dx[:, e * C : (e + 1) * C], sums[:, e, :], gate_first[:, e * C : (e + 1) * C], MULT)
-            else:
-                late.append((e, acc))
-        for h in range(2):
-            nc.scalar.copy(ds[:, h * C : (h + 1) * C], shared[h][:])
-        for e, acc in late:
-            nc.vector.tensor_tensor(dx[:, e * C : (e + 1) * C], acc[:], gate_last[:, (e - POOLED) * C : (e - POOLED + 1) * C], MULT)
+        turned = bank(0, "turned")
 
-        def pick(h, r):
-            t = keep.tile([P, C], F32, name="pick%d_%d" % (h, r))
-            nc.vector.tensor_copy(t[:], dx[:].indirect(pos_sb[r][:, h * C // 16 : (h + 1) * C // 16]))
-            return t
-
-        turned = bank(4, "turned")
-
-        def turn(term, n):
+        def turn(term, start, stop):
             for b in range(BLOCKS):
-                nc.tensor.matmul(turned[:, block(b)], term[:, block(b)], ident[:], start=(n == 0 and b == 0), stop=(n == 2 and b == BLOCKS - 1), is_transpose=True)
+                nc.tensor.matmul(turned[:, block(b)], term[:, block(b)], ident[:], start=(start and b == 0), stop=(stop and b == BLOCKS - 1), is_transpose=True)
 
-        def pool_add(n, x, y):
-            t = keep.tile([P, C], F32, name="part%d" % n)
-            nc.gpsimd.tensor_tensor(t[:], x, y, ADD)
-            return t
+        def add_on_gpsimd(r, total, term):
+            new_total = kept([P, HALF], F32, "total0_%d" % r)
+            nc.gpsimd.tensor_tensor(new_total[:], total, term, ADD)
+            return new_total[:]
 
-        turn(ds[:, C:T], 0)
-        turn(pick(1, 0)[:], 1)
-        part = pool_add(0, ds[:, 0:C], pick(0, 0)[:])
-        turn(pick(1, 1)[:], 2)
-        staged = keep.tile([P, C], F32, name="staged")
+        turn(ds[1], True, False)
+        turn(pick(1, 0), False, False)
+        total = add_on_gpsimd(0, ds[0], pick(0, 0))
+        turn(pick(1, 1), False, True)
+        staged = kept([P, HALF], F32, "staged")
         nc.scalar.copy(staged[:], turned[:])
-        back = bank(5, "back")
+        partial = bank(1, "partial")
         for b in range(BLOCKS):
-            nc.tensor.transpose(back[:, block(b)], staged[:, block(b)], ident[:])
-        part = pool_add(1, part[:], pick(0, 1)[:])
-        part = pool_add(2, part[:], pick(0, 2)[:])
-        nc.sync.dma_start(out[:, 0:C], part[:])
-        last = pick(1, 2)
+            nc.tensor.transpose(partial[:, block(b)], staged[:, block(b)], ident[:])
+        total = add_on_gpsimd(1, total, pick(0, 1))
+        total = add_on_gpsimd(2, total, pick(0, 2))
+        nc.sync.dma_start(out[:, 0:HALF], total)
+
+        last_pick = pick(1, 2)
         for i in range(2):
-            cols = slice(i * C // 2, (i + 1) * C // 2)
-            total = keep.tile([P, C // 2], F32, name="total%d" % i)
-            nc.vector.tensor_tensor(total[:], back[:, cols], last[:, cols], ADD)
-            nc.scalar.dma_start(out[:, C + i * C // 2 : C + (i + 1) * C // 2], total[:])
+            cols = slice(i * HALF // 2, (i + 1) * HALF // 2)
+            quarter = kept([P, HALF // 2], F32, "total1_%d" % i)
+            nc.vector.tensor_tensor(quarter[:], partial[:, cols], last_pick[:, cols], ADD)
+            nc.scalar.dma_start(out[:, HALF + cols.start : HALF + cols.stop], quarter[:])

from contextlib import ExitStack

import concourse.mybir as mybir
from concourse.masks import make_identity

K, T, E, C, N = 128, 1024, 6, 512, 1536
SHARED = E
LAST = E - 1
SLOTS = E * C
FLOPS = 2 * K * N * (SLOTS + T)

P = 128
PACK = 4
PASSES = N // (P * PACK)
PER_COLUMN = 16
HALF = T // 2
BLOCKS = HALF // P

STACK_ROW = (0, 8, 28)
MOVED_ROWS = (0, 112, 100)
SCALE_PIECE = 768
RUN = 4
STAGGERED = 3

WORDS_BYTES = C * 4
RAW_BYTES = PASSES * PACK * K * 4

F32 = mybir.dt.float32
BF16 = mybir.dt.bfloat16
I32 = mybir.dt.int32
U32 = mybir.dt.uint32
U16 = mybir.dt.uint16
U8 = mybir.dt.uint8
E4M3 = mybir.dt.float8_e4m3fn_x4
E5M2 = mybir.dt.float8_e5m2_x4
MULT = mybir.AluOpType.mult
ADD = mybir.AluOpType.add


def tile_moe_bds_lin_none_kernel(tc, dy_words, dy_scales, w, gate, offs, pos1, pos2, pos3, out):
    nc = tc.nc
    with ExitStack() as ctx:
        lists = ctx.enter_context(tc.tile_pool(name="lists", bufs=1))
        keep = ctx.enter_context(tc.tile_pool(name="keep", bufs=1))
        reuse = ctx.enter_context(tc.tile_pool(name="reuse", bufs=1))
        psum = ctx.enter_context(tc.psum_pool(name="psum", bufs=1))

        def bank(i, name):
            return psum.tile([P, C], F32, name=name, tag="bank%d" % i)

        def kept(shape, dtype, name):
            return keep.tile(shape, dtype, name=name, align_bytes=64)

        def placed(shape, dtype, name, offset):
            return reuse.tile(shape, dtype, name=name, align_bytes=64, offset=offset)

        offs_sb = lists.tile([P, SLOTS // PER_COLUMN], U16, name="offs_sb")
        pos_sb = [lists.tile([P, T // PER_COLUMN], U16, name="pos%d_sb" % r) for r in range(3)]

        words = [kept([P, T], I32, "words%d" % a) for a in range(PASSES)]
        token_stack = kept([P, T], U8, "token_stack")
        slot_stack = kept([P, SLOTS], U8, "slot_stack")
        token_plane = [token_stack] + [kept([P, T], U8, "token_plane%d" % a) for a in range(1, PASSES)]
        slot_plane = [slot_stack] + [kept([P, SLOTS], U8, "slot_plane%d" % a) for a in range(1, PASSES)]

        raw_at = [e * RAW_BYTES for e in range(LAST)] + [E * RAW_BYTES, LAST * RAW_BYTES]
        w_raw = [placed([P, PASSES, PACK, K], F32, "w_raw%d" % e, raw_at[e]) for e in range(E + 1)]
        first_pass = [kept([P, C], U32, "first_pass%d" % e) for e in range(LAST - 1)]
        first_pass.append(placed([P, C], U32, "first_pass_4", raw_at[0] + 2 * WORDS_BYTES))
        first_pass.append(placed([P, C], U32, "first_pass_last", raw_at[LAST]))
        later = [placed([P, 2, C], U32, "later%d" % e, raw_at[e])[:] for e in range(STAGGERED)]
        late_at = raw_at[LAST] + WORDS_BYTES
        late = placed([P, E - STAGGERED, 2, C], U32, "late", late_at)
        later += [late[:, e, :, :] for e in range(E - STAGGERED)]
        slot_words = [[first_pass[e][:], later[e][:, 0, :], later[e][:, 1, :]] for e in range(E)]

        drained_at = late_at + (E - STAGGERED) * 2 * WORDS_BYTES
        w_bf = [kept([P, PASSES * K * PACK], BF16, "w_bf%d" % e) for e in range(LAST)]
        w_bf.append(placed([P, PASSES * K * PACK], BF16, "w_bf_last", drained_at))
        w_bf.append(kept([P, PASSES * K * PACK], BF16, "w_bf_shared"))
        drained = placed([P, LAST + 2, C], F32, "drained", drained_at)
        ds = [drained[:, LAST + h, :] for h in range(2)]
        w_codes = [kept([P, PASSES * K], U32, "w_codes%d" % e) for e in range(E)]
        w_codes.append(placed([P, PASSES * K], U32, "w_codes_shared", raw_at[LAST]))
        w_scales = [kept([P, PASSES * K], U8, "w_scales%d" % e) for e in range(E + 1)]

        gate_sb = kept([P, SLOTS], F32, "gate_sb")
        ident = kept([P, P], F32, "ident")
        dx = kept([P, SLOTS], F32, "dx")

        def load_words(a):
            nc.sync.dma_start(words[a][:], dy_words[a].rearrange("p t d -> p (t d)").bitcast(I32))

        def load_w(e):
            nc.sync.dma_start(w_raw[e][:], w[e].rearrange("(a p j) k -> p a j k", a=PASSES, j=PACK))

        def move_plane(plane, stack, a):
            rows = MOVED_ROWS[a]
            nc.gpsimd.dma_start(plane[0:rows, :].bitcast(I32), stack[STACK_ROW[a] : STACK_ROW[a] + rows, :].bitcast(I32))

        nc.sync.dma_start(offs_sb[:], offs)
        load_words(0)
        scale_rows = dy_scales.rearrange("a f t -> (a f) t").bitcast(I32)
        for q in range(4):
            for upper in range(2):
                rows = scale_rows[4 * (q + upper) : 4 * (q + upper) + 32, :].rearrange("(g f) t -> g f t", g=2)
                first = 32 * q + 16 * upper
                nc.sync.dma_start(token_stack[first : first + 16, :].bitcast(I32), rows[:, 8 * upper : 8 * upper + 8, :])
        for a in range(1, PASSES):
            nc.vector.memset(token_plane[a][:].bitcast(I32), 0)
            nc.vector.memset(slot_plane[a][:].bitcast(I32), 0)
        make_identity(nc, ident[:])
        for a in range(1, PASSES):
            move_plane(token_plane[a], token_stack, a)
        load_w(0)
        load_words(1)
        load_words(2)
        for e in range(1, E + 1):
            load_w(e)
        nc.sync.dma_start(gate_sb[:], gate)
        for r, pos in enumerate((pos1, pos2, pos3)):
            nc.sync.dma_start(pos_sb[r][:], pos)

        def round_w(e):
            nc.scalar.copy(
                w_bf[e][:].rearrange("p (a c i j) -> p a c j i", a=PASSES, i=RUN, j=PACK),
                w_raw[e][:].rearrange("p a j (c i) -> p a c j i", i=RUN),
            )

        def quantise(e):
            for lo, hi in ((0, 2 * K), (2 * K, PASSES * K)):
                nc.vector.quantize_mx(out=w_codes[e][:, lo:hi].bitcast(E4M3), scales=w_scales[e][:, lo:hi], in_=w_bf[e][:, PACK * lo : PACK * hi])

        def entries(list_sb, lo, hi):
            return list_sb[:, lo // PER_COLUMN : hi // PER_COLUMN]

        def gather_words(e, a):
            nc.vector.tensor_copy(slot_words[e][a], words[a][:].bitcast(U32).indirect(entries(offs_sb, e * C, (e + 1) * C)))

        def multiply(acc, e, moving, planes):
            for a in range(PASSES):
                nc.tensor.matmul_mx(
                    out=acc[:],
                    lhsT=w_codes[e][:, a * K : (a + 1) * K].bitcast(E4M3),
                    lhsT_scale=w_scales[e][:, a * K : (a + 1) * K],
                    rhs=moving[a].bitcast(E5M2),
                    rhs_scale=planes[a],
                    start=(a == 0),
                    stop=(a == PASSES - 1),
                )

        for e in range(LAST - 1):
            gather_words(e, 0)
        for lo in range(0, SLOTS, SCALE_PIECE):
            nc.vector.tensor_copy(slot_stack[:, lo : lo + SCALE_PIECE], token_stack[:].indirect(entries(offs_sb, lo, lo + SCALE_PIECE)))
        for a in range(1, PASSES):
            move_plane(slot_plane[a], slot_stack, a)
        for e in range(E + 1):
            round_w(e)
        gather_words(LAST - 1, 0)

        for e in range(E):
            slots = slice(e * C, (e + 1) * C)
            if e < STAGGERED:
                quantise(e)
            elif e == STAGGERED:
                for other in range(STAGGERED, E):
                    quantise(other)
            for a in range(0 if e == LAST else 1, PASSES):
                gather_words(e, a)
            acc = bank(e, "acc%d" % e)
            multiply(acc, e, slot_words[e], [slot_plane[a][:, slots] for a in range(PASSES)])
            if e < LAST:
                nc.scalar.copy(drained[:, e, :], acc[:])
                nc.gpsimd.tensor_tensor(dx[:, slots], drained[:, e, :], gate_sb[:, slots], MULT)
            else:
                quantise(SHARED)
                nc.vector.tensor_tensor(dx[:, slots], acc[:], gate_sb[:, slots], MULT)

        for h in (1, 0):
            tokens = slice(h * HALF, (h + 1) * HALF)
            acc = bank(E + h, "acc_shared%d" % h)
            multiply(acc, SHARED, [words[a][:, tokens] for a in range(PASSES)], [token_plane[a][:, tokens] for a in range(PASSES)])
            nc.scalar.copy(ds[h], acc[:])

        def pick(h, r):
            picked = kept([P, HALF], F32, "pick%d_%d" % (h, r))
            nc.vector.tensor_copy(picked[:], dx[:].indirect(entries(pos_sb[r], h * HALF, (h + 1) * HALF)))
            return picked[:]

        def block(b):
            return slice(b * P, (b + 1) * P)

        turned = bank(0, "turned")

        def turn(term, start, stop):
            for b in range(BLOCKS):
                nc.tensor.matmul(turned[:, block(b)], term[:, block(b)], ident[:], start=(start and b == 0), stop=(stop and b == BLOCKS - 1), is_transpose=True)

        def add_on_gpsimd(r, total, term):
            new_total = kept([P, HALF], F32, "total0_%d" % r)
            nc.gpsimd.tensor_tensor(new_total[:], total, term, ADD)
            return new_total[:]

        turn(ds[1], True, False)
        turn(pick(1, 0), False, False)
        total = add_on_gpsimd(0, ds[0], pick(0, 0))
        turn(pick(1, 1), False, True)
        staged = kept([P, HALF], F32, "staged")
        nc.scalar.copy(staged[:], turned[:])
        partial = bank(1, "partial")
        for b in range(BLOCKS):
            nc.tensor.transpose(partial[:, block(b)], staged[:, block(b)], ident[:])
        total = add_on_gpsimd(1, total, pick(0, 1))
        total = add_on_gpsimd(2, total, pick(0, 2))
        nc.sync.dma_start(out[:, 0:HALF], total)

        last_pick = pick(1, 2)
        for i in range(2):
            cols = slice(i * HALF // 2, (i + 1) * HALF // 2)
            quarter = kept([P, HALF // 2], F32, "total1_%d" % i)
            nc.vector.tensor_tensor(quarter[:], partial[:, cols], last_pick[:, cols], ADD)
            nc.scalar.dma_start(out[:, HALF + cols.start : HALF + cols.stop], quarter[:])
